import numpy as np, ml_dtypes
CORES = [25,29,65,69,153,157,193,197]
N = 8
BF = ml_dtypes.bfloat16
S, NM, L, RO, TAU = 1024, 2048, 256, 4, 6
ST, C0, LN = S // L, 16 - RO, NM.bit_length() - 1
def pack(nm, st, kd, ac, fu):
    return np.where(fu, 1 + 2048 * nm + 32 * st + 16 * kd + ac, 0)
def done(e, x, w, kp):
    return {"ent": np.ascontiguousarray(e.reshape(N, 128, S)).astype(np.int32), "feat": np.ascontiguousarray(x.reshape(N, 128, NM)).astype(np.float32).astype(BF),
            "wt": np.ascontiguousarray(w.reshape(N, 128, 1)).astype(np.int32), "kap": np.ascontiguousarray(kp.reshape(N, 128, 1)).astype(np.int32)}
def pooled(rng, n, other):
    pool = rng.integers(0, NM, (8, 16, n)); pool[..., 0] = rng.choice(np.array([0, NM - 1]), (8, 16))
    j = (n * rng.random((N, 8, 16, S)) ** 2).astype(np.int64)
    v = pool[np.arange(8)[:, None, None], np.arange(16)[None, :, None], j]
    return np.where(rng.random(v.shape) < other, rng.integers(0, NM, v.shape), v)
def parts(rng, n, other):
    sh = (N, 8, 16, S); nm = pooled(rng, n, other)
    st = rng.integers(0, 64, sh); kd = (rng.random(sh) < 0.45).astype(np.int64); ac = rng.integers(0, 16, sh); fu = rng.random(sh) < 0.8
    x = (64 * rng.random((N, 8, 16, NM)) ** 2).astype(np.int64)
    return nm, st, kd, ac, fu, x, rng.integers(0, 256, (N, 8, 16)), rng.integers(0, 256, (N, 8, 16))
def setup_inputs(rng):
    nm, st, kd, ac, fu, x, w, kp = parts(rng, 24, 0.3)
    return done(pack(nm, st, kd, ac, fu), x, w, kp)
def setup_inputs_spread(rng):
    sh = (N, 8, 16, S)
    nm = np.exp2(LN * rng.random(sh)).astype(np.int64) - 1; nm = np.where(rng.random((1, 8, 16, 1)) < 0.5, NM - 1 - nm, nm)
    st = np.exp2(6 * rng.random(sh)).astype(np.int64) - 1; st = np.where(rng.random(sh) < 0.5, 63 - st, st)
    kd = (rng.random(sh) < rng.choice(np.array([0.1, 0.4, 0.8]), (N, 8, 1, 1))).astype(np.int64)
    fu = rng.random(sh) < rng.random((N, 8, 1, S))
    x = (np.exp2(6 * rng.random((N, 8, 1, NM))) * rng.random((N, 8, 16, NM))).astype(np.int64)
    w = np.exp2(8 * rng.random((N, 8, 16))).astype(np.int64) - 1; kp = 256 - np.exp2(8 * rng.random((N, 8, 16))).astype(np.int64)
    return done(pack(nm, st, kd, rng.integers(0, 16, sh), fu), x, w, kp)
def at_ends(rng, hi):
    o = np.argsort(rng.random((N, 8, 16)), axis=-1)
    return np.where(o < 11, hi * rng.integers(0, 2, o.shape), rng.integers(0, hi + 1, o.shape))
def setup_inputs_ends(rng):
    sh = (N, 8, 16, S); top = 2048 * NM
    z = 32 * 63 * rng.integers(0, 2, sh) + 15 * rng.integers(0, 2, sh) + 1
    e = np.where(rng.random(sh) < 0.28, 2048 * rng.integers(0, NM, sh) + z, top * rng.integers(0, 2, sh))
    k = rng.random((N, 8, 1, S)); last = 2048 * (NM - 1) + z
    e = np.where(k < 0.41, 16 + z, e); e = np.where(k < 0.37, z, e); e = np.where(k < 0.33, last, e)
    e = np.where(k < 0.26, 0, e); e = np.where(k < 0.16, top, e)
    x = 63 * (rng.random((N, 8, 16, NM)) < 0.2).astype(np.int64); x[..., NM - 1] = 63; x[..., 0] = 0
    w = at_ends(rng, 255); kp = at_ends(rng, 255); w[0, 7] = 255; w[N - 1, 7] = 255
    for c in [0, ST] + list(range(S - ST, S)): e[:, 7, :, c] = last[:, 7, :, c]
    u = 16 * 63 * 255 & 4095
    for m in (8, 15): e[0, 7, :, ((u * u >> 5) + int(kp[N - 1, 7, m]) * u) & (S - 1)] = top
    return done(e, x, w, kp)
def setup_inputs_corners(rng):
    nm, st, kd, ac, fu, x, w, kp = parts(rng, 6, 0.1); sh = kd.shape
    o = rng.permutation(8); md = o[(np.arange(8)[None, :] + (np.arange(N)[:, None] & 1)) & 7]; m4 = md[:, :, None, None]
    kd = np.where(m4 == 0, 1, np.where(m4 == 1, 0, kd)); fu = fu | (m4 == 1)
    fu = np.where(m4 == 2, rng.random((N, 8, 1, S)) < 0.5, fu)
    ac = np.where(m4 == 3, C0 - TAU - 1 + rng.integers(0, RO + 1, sh), ac); kd = np.where(m4 == 3, (rng.random(sh) < 0.7).astype(np.int64), kd)
    st = np.where(m4 == 4, 63 * rng.integers(0, 2, sh), st); st = np.where(m4 == 7, 31, st)
    kd = np.where(m4 == 6, ((np.arange(S)[None, :] & 15) != np.arange(16)[:, None]).astype(np.int64), kd); fu = fu | (m4 == 6)
    x = np.where(m4 == 5, 63, x); m3 = md[:, :, None]
    w = np.where(m3 == 4, 0, np.where(m3 == 7, 255, w)); kp = np.where(m3 == 6, 0, np.where(m3 == 7, 255, kp))
    return done(pack(nm, st, kd, ac, fu), x, w, kp)
def setup_inputs_ties(rng):
    nm, st, kd, ac, fu, x, w, kp = parts(rng, 3, 0.02); sh = st.shape
    st = rng.integers(0, 63, (1, 8, 16, 1)) + rng.integers(0, 2, sh)
    ac = rng.choice(np.array([0, C0 - TAU - 1, C0 - TAU, C0 - TAU + 1, C0, 15]), sh); fu = rng.random(sh) < 0.9
    e = pack(nm, st, kd, ac, fu)
    w[..., 0] |= 1; kp = np.argsort(rng.random((N, 8, 256)), axis=-1)[..., :16]
    nn = rng.integers(0, NM, (N, 8, 16)); c = np.zeros((N, 8, 16), np.int64)
    for r in range(N):
        for g in range(8):
            n = int(nn[r, g, 0])
            if int(np.add.reduce(w[r, g] * x[r, g, :, n])) & 1 == 0: x[r, g, 0, n] ^= 1
            u = int(np.add.reduce(w[r, g] * x[r, g, :, n])) & 4095
            c[r, g] = ((u * u >> 5) + kp[r, g] * u) & (S - 1)
    for r in range(N):
        for g in range(8):
            q = (r + 1) % N; l = min(i for i in range(17) if not np.any(c[r - 1, g] == ST * i))
            s = rng.integers(0, 64, 16); own = pack(nn[r, g], s, (np.arange(16) > 0).astype(np.int64), rng.integers(0, 16, 16), True)
            e[r, g, :, ST * l] = own
            d = rng.integers(1, 4, 16); m = np.sort(rng.permutation(16)[:2]); d[m] = np.array([1, 0]) if (r + g) & 1 else np.array([0, 1])
            miss = np.argsort(rng.random((16, 16)), axis=0) < d[None, :]
            hit = pack(nn[r, g][:, None], s[:, None] ^ rng.integers(1, 64, (16, 16)), rng.integers(0, 2, (16, 16)), rng.integers(0, 16, (16, 16)), True)
            no = np.where(rng.random((16, 16)) < 0.5, 0, (((own - 1) >> 4) << 4)[:, None] + 1 + rng.integers(0, 16, (16, 16)))
            e[q, g][:, c[r, g]] = np.where(miss, no, hit)
    return done(e, x, w, kp)
def gone(v, c):
    return np.where((((37 * c + v) >> 3) & 7) == 0, v ^ 8, v)
def setup_inputs_crowd(rng):
    nm, st, kd, ac, fu, x, w, kp = parts(rng, 8, 0.2)
    e = np.take_along_axis(pack(nm, st, kd, ac, fu), rng.integers(0, 24, (N, 8, 1, S)), 3)
    kp[:, ::2] = kp[:, ::2, :1]
    h = int(rng.integers(0, 8)); kp[:, h] = 0; w[:, h] = 0; w[:, h, 0] = 1; w[:, h, 15] = 64
    cols = ST * np.arange(1, L); sh = (16, L - 1)
    for r in range(N):
        q = (r + 1) % N; o = rng.permutation(4096); c = (o * o >> 5) & (S - 1)
        first = np.unique(c, return_index=True)[1]; first = first[c[first] % ST != 0]
        u = o[rng.permutation(first)[:L - 1]]; p = (u * u >> 5) & (S - 1)
        names = rng.permutation(NM)[:L - 1]; x[r, h, 0, names] = u & 63; x[r, h, 15, names] = u >> 6
        it = rng.random(sh) < 0.4; it[0] = True; it[15] = True
        a = pack(np.where(it, names[None, :], rng.integers(0, NM, sh)), rng.integers(0, 64, sh), 1 - it.astype(np.int64), rng.integers(0, C0 - TAU, sh), True)
        b = pack(gone(rng.integers(0, NM, sh), p[None, :]), rng.integers(0, 64, sh), 1, rng.integers(0, C0 - TAU, sh), True)
        full = rng.random(L - 1) < 0.5; full[-1] = True
        e[r, h][:, cols] = a
        e[q, h][:, p] = np.where(full[None, :], b, a)
    e[:, h, :, 0] = pack(gone(rng.integers(0, NM, 16), 0), rng.integers(0, 64, 16), 1, rng.integers(0, C0 - TAU, 16), True)[None, :]
    return done(e, x, w, kp)
def check_inputs(d):
    bad = []
    for k, lo, hi in (("ent", 0, 2048 * NM), ("feat", 0, 63), ("wt", 0, 255), ("kap", 0, 255)):
        v = np.asarray(d[k]).astype(np.float64)
        if not (np.min(v) >= lo and np.max(v) <= hi): bad.append("range of " + k)
        elif np.any(v != np.floor(v)): bad.append("whole numbers in " + k)
    return bad
def item(a):
    return (a > 0) & ((((a - 1) >> 4) & 1) == 0)
def asleep(a, clock):
    return (a > 0) & ((((a - 1) >> 4) & 1) == 1) & (clock - ((a - 1) & 15) > TAU)
def stay(a, site, clock):
    return np.where(asleep(a, clock) & ((((37 * site + ((a - 1) >> 11)) >> 3) & 7) != 0), 0, a)
def meet(a, b, clock):
    same = (a > 0) & (b > 0) & (((a - 1) >> 11) == ((b - 1) >> 11)); big = np.maximum(a, b)
    wake = same & asleep(big, clock) & item(np.minimum(a, b))
    big = np.where(wake, (((big - 1) >> 4) << 4) + clock + 1, big)
    return np.where(same, big, np.where((a == 0) & ~asleep(b, clock), b, a)), np.where(same, big, np.where((b == 0) & ~asleep(a, clock), a, b))
def reference(ent, feat, wt, kap):
    E = ent.astype(np.int64).reshape(N, 8, 16, S); X = feat.astype(np.float32).astype(np.int64).reshape(N, 8, 16, NM)
    w = wt.astype(np.int64).reshape(N, 8, 16, 1); kp = kap.astype(np.int64).reshape(N, 8, 16, 1); A = [0] * N
    for t in range(RO):
        clock = C0 + t; lane = ST * np.arange(L) + t % ST; new = E.copy(); called = []
        for r in range(N):
            q = (r + 1 + t % (N - 1)) % N
            a = E[r][:, :, lane]
            x = np.take_along_axis(X[r], np.maximum((a - 1) >> 11, 0).reshape(8, 1, 16 * L), 2).reshape(8, 16, 16, L)
            y = np.max(np.where(item(a)[:, None], x, 0), axis=2)
            u = np.add.reduce(w[r] * y, axis=1)[:, None, :] & 4095
            e = ((u * u >> 5) + kp[r] * u + A[r]) & (S - 1)
            cand = np.take_along_axis(E[q], e.reshape(8, 1, 16 * L), 2).reshape(8, 16, 16, L) - 1
            own = a[:, :, None, :] - 1
            score = np.add.reduce((((cand >> 11) == (own >> 11)) & ((cand >> 4) != (own >> 4))).astype(np.int64), axis=1)
            p = np.take_along_axis(e, np.argmax(score, axis=1)[:, None, :], 1)
            win = np.zeros((8, L), bool)
            for g in range(8): win[g, np.unique(p[g, 0], return_index=True)[1]] = True
            b = np.take_along_axis(E[q], p, 2)
            na, nb = meet(stay(a, lane[None, None, :], clock), stay(b, p, clock), clock)
            new[r][:, :, lane] = np.where(win[:, None, :], na, a)
            called.append((q, p[:, 0], win, nb)); A[r] = int(np.count_nonzero(win)) & 31
        for q, p, win, nb in called:
            for g in range(8): new[q, g][:, p[g, win[g]]] = nb[g][:, win[g]]
        E = new
    return {"yent": E.reshape(N, 128, S).astype(np.float32)}

from concourse.mybir import AluOpType as ALU, ActivationFunctionType as AF

NR = 4
EMP = 4096.0 * 2050
P23, P24 = float(1 << 23), float(1 << 24)
GS = 5
SQ = 6
LAT = {"a": 5.0, "u": 4.5, "c": 4.5, "n": 5.0}
WAKE = 0.1
SLACK = 0.03
PIECES = 2

SCRATCH = {}


def _sb(dtype, **cols):
    for n in cols:
        SCRATCH[n] = ("sbuf", [128, cols[n]], dtype)


_sb("int32", entx=1024, R=1280, wti=1, kpi=1, ci=1024, ci2=1024, pmi=16, pmj=16, xv=256, xh=256)
_sb("bfloat16", fx=2064, one=128, blka=128, blk=128, blkb=128, zer=256, sel=2048, wsel=2048, tri=2048, dlt=256, rA=256, rK=256, sgm=512)
_sb("float32", wtf=1, iot=1024, Ct0=1024, Ct1=1024, Ct2=1024, Ct3=1024, allf=128, pmf=16, x16=16, cmk=16, c15=1, mio=256, lio=512,
    lbl=256, dma_=256, DM=256, KM=256, kcol=1, xs=256)
_sb("uint16", lst=16, off=256, eu=256, e16=16, ebc=256, pos=16)
_sb("int32", k1=256, ui=16, ub=16, uq=16, us=16, ei=256, em=256, oc=512, ky=16, kk=16, es=16, er=16, ti=1)
_sb("float32", pr=256, acol=1, ep=256, D=4096, mx=64, m2=32, ku=16, erf=16, wacc=1, px=256, ps=256, pf=16)
_sb("bfloat16", Yg=4096, Ys=4096, X=4096, Y=4096, NM=4096, EQ=4096)
_sb("int32", qa=256, za=256, l5a=256, ita=256, bI=256, qb=256, zb=256, l5b=256, itb=256, hi=256)
_sb("float32", aw=256, aP=256, zda=256, zdb=256, ca=256, bs=256, wbx=256, pb=256, rr=256, Xd=256, na1=256, nb1=256, na3=256, nbA=256,
    a1=256, nb=256, yo=1024, xo=256)
for _n in ("pk0", "pk1", "pu", "pc", "pm", "t1", "t2", "t3"):
    SCRATCH[_n] = ("psum", [128, 512], "float32")
STEP = {"a": 264, "u": 32, "c": 4, "n": 256}
PART = {}
MSG = {"a": (258, "int32"), "u": (32, "float32"), "c": (1, "int32"), "n": (256, "int32")}
SEMAPHORES = ["qv", "qs", "qp", "qg", "ld0", "ld1", "ld2", "ld3", "oc0", "oc1", "oc2", "oc3", "st", "lsem"]
for _t in range(NR):
    for _m in MSG:
        if _m == "c" and _t == NR - 1:
            continue
        for _s in "sl":
            SCRATCH[_s + _m] = ("sbuf", [128, NR * STEP[_m]], MSG[_m][1])
            PART["%s%s%d" % (_s, _m, _t)] = (_s + _m, _t * STEP[_m], MSG[_m][0])
        SEMAPHORES.append("%s%d" % (_m, _t))
for _n, _b, _c in (("v1", "t1", 0), ("v2", "t1", 256), ("v3", "t2", 0), ("v4", "t2", 256), ("v5", "t3", 0), ("v6", "t3", 256),
                   ("cbp", "pk0", 0), ("dbp", "pk0", 256), ("dap", "pm", 256), ("nsp", "pk1", 0), ("wnp", "pk1", 256), ("bPp", "pm", 0), ("dp", "pu", 256), ("ctl", "pc", 256)):
    PART[_n] = (_b, _c, 256)


def bits(m):
    return bin(m).count("1")


def relays(topo, T, src, dst):
    return [c for c in topo.cores_of(src) if topo.may_write(c, dst) and topo.die(c) == topo.die(src) and T.rank_of(c) is None]


def route(topo, T, src, dst, m, t):
    w = MSG[m][0]
    if topo.may_write(src, dst):
        return [(None, 0, w)]
    rl = relays(topo, T, src, dst)
    if w < 64:
        return [(rl[1 if m == "u" else 0], 0, w)]
    return [(rl[0], 0, 128), (rl[1], 128, w)]


def target(T, rank, m, t):
    n = len(T.cores)
    s = 1 + t % (n - 1)
    return (rank + s) % n if m in "au" else (rank - s) % n


def source(T, rank, m, t):
    n = len(T.cores)
    s = 1 + t % (n - 1)
    return (rank - s) % n if m in "au" else (rank + s) % n


def hand_on(g, core, T, topo):
    sent = 0
    mine = [r for r, c in enumerate(T.cores) if c in topo.cores_of(core)]
    if not mine:
        return
    for m, t in plan(T)[2]:
        for r in mine:
            src, dst = T.cores[r], T.cores[target(T, r, m, t)]
            for rl, lo, hi in route(topo, T, src, dst, m, t):
                if rl != core:
                    continue
                b, at = T["l" + m], STEP[m] * t
                sem = T.sem["%s%d" % (m, t)]
                g.wait_ge(sem, bits(topo.mask(src, core)))
                rid, pid = topo.addr(dst, core)
                mk = topo.mask(core, dst)
                g.remote_dma(b[:, at + lo:at + hi], b[:, at + lo:at + hi], sem, T.sem.lsem, pid, rid, mk)
                sent += bits(mk)
    if sent:
        g.wait_ge(T.sem.lsem, sent)


def B(name, lo=0, hi=None, st=1):
    if name in PART:
        b, at, w = PART[name]
        return (b, at + lo, at + (w if hi is None else hi), st)
    return (name, lo, SCRATCH[name][1][1] if hi is None else hi, st)


def width(x):
    return (x[2] - x[1] + x[3] - 1) // x[3]


def meets(a, b):
    if a[2] <= b[1] or b[2] <= a[1]:
        return False
    return not (a[3] == b[3] and a[3] > 1 and (a[1] - b[1]) % a[3])


def covers(a, b):
    return a[1] <= b[1] and b[2] <= a[2] and (a[3] == 1 or (a[3] == b[3] and (a[1] - b[1]) % a[3] == 0))


def links(ops):
    acc, out = {}, []
    for i, o in enumerate(ops):
        pre = set(o["after"])
        for wr, lst in ((False, o["r"]), (True, o["w"])):
            for x in lst:
                ps = SCRATCH[x[0]][0] == "psum"
                for (y, w2, j) in acc.get(x[0], []):
                    if j == i:
                        continue
                    if ps and (ops[j]["q"] != o["q"] or o["q"] == "p"):
                        pre.add(j)
                    elif (wr or w2) and meets(x, y):
                        pre.add(j)
        for x in o["w"]:
            acc[x[0]] = [a for a in acc.get(x[0], []) if a[2] == i or not covers(x, a[0]) or (SCRATCH[x[0]][0] == "psum" and ops[a[2]]["q"] != o["q"])]
            acc[x[0]].append((x, True, i))
        for x in o["r"]:
            acc.setdefault(x[0], []).append((x, False, i))
        out.append(sorted(pre))
    return out


def arrange(ops, pre, wake):
    n = len(ops)
    suc = [[] for _ in range(n)]
    for i in range(n):
        for j in pre[i]:
            suc[j].append(i)
    prio = [0.0] * n
    for i in range(n - 1, -1, -1):
        prio[i] = ops[i]["dur"] + (0.0 if ops[i]["q"] == "p" else wake) + max([prio[k] for k in suc[i]] + [0.0])
    left = [len(p) for p in pre]
    est = [0.0] * n
    ready = [i for i in range(n) if left[i] == 0]
    free, seq = {}, []
    while ready:
        st = {i: max(free.get(ops[i]["q"], 0.0), est[i]) for i in ready}
        first = min(ready, key=lambda i: (st[i], -prio[i]))
        q, lim = ops[first]["q"], st[first] + SLACK
        i = max([k for k in ready if ops[k]["q"] == q and st[k] <= lim], key=lambda k: (prio[k], -k))
        if q is None:
            i = first
        ready.remove(i)
        seq.append(i)
        end = st[i] + ops[i]["dur"]
        if q is not None:
            free[q] = st[i] + 0.06 if ops[i]["kind"] == "dma" else end
        for k in suc[i]:
            est[k] = max(est[k], end if q == "p" and ops[k]["q"] == "p" else end + wake)
            left[k] -= 1
            if left[k] == 0:
                ready.append(k)
    return seq


def record(T):
    ops, where = [], {}
    CY, G, SC = 0.001, 1.5, 3.0

    def put(kind, q, fn, r, w, dur, after=(), **more):
        d = {"kind": kind, "q": q, "fn": fn, "r": list(r), "w": list(w), "dur": dur, "after": list(after)}
        d.update(more)
        ops.append(d)

    def ap(x):
        name, lo, hi, st = x
        return T[name][:, lo:hi:st] if st != 1 else T[name][:, lo:hi]

    def two(*xs):
        return 0.5 if all(SCRATCH[x[0]][2] in ("bfloat16", "uint16") for x in xs) else 1.0

    def vd(n, k=1.0):
        return max(64.0, n * k) * CY

    def ts(o, a, s1, op0, s2=None, op1=None, sc=None):
        d = vd(width(a), two(o, a))
        r = [a] if sc is None else [a, sc]
        if op1 is None:
            put("run", "v", lambda e: e.tensor_scalar(ap(o), ap(a), s1 if sc is None else ap(sc), None, op0), r, [o], d)
        else:
            put("run", "v", lambda e: e.tensor_scalar(ap(o), ap(a), s1 if sc is None else ap(sc), s2, op0, op1), r, [o], d)

    def tt(o, a, b, op):
        k = 1.0 if "psum" in (SCRATCH[a[0]][0], SCRATCH[b[0]][0]) else 2.0
        put("run", "v", lambda e: e.tensor_tensor(ap(o), ap(a), ap(b), op), [a, b], [o], vd(width(a), k))

    def cp(o, a):
        put("run", "v", lambda e: e.tensor_copy(ap(o), ap(a)), [a], [o], vd(width(a), two(o, a)))

    def ms(o, c):
        put("run", "v", lambda e: e.memset(ap(o), c), [], [o], vd(width(o), two(o)))

    def pick(o, win, off, b=None, op=None):
        r, d = [win, off] + ([b] if b is not None else []), 0.06 + 16 * width(off) * G * CY
        if b is None:
            put("run", "v", lambda e: e.tensor_copy(ap(o), ap(win).indirect(ap(off))), r, [o], d)
        else:
            put("run", "v", lambda e: e.tensor_tensor(ap(o), ap(win).indirect(ap(off)), ap(b), op), r, [o], d)

    def scatter(win, off, a):
        put("run", "v", lambda e: e.tensor_copy(ap(win).indirect(ap(off)), ap(a)), [a, off], [win], 0.06 + width(a) * SC * CY)

    def scan(o, m, a):
        put("run", "v", lambda e: e.tensor_tensor_scan(ap(o), ap(m), ap(a), 0.0, ALU.mult, ALU.max), [m, a], [o], vd(width(a), two(o, m, a)))

    def act(o, a, f, bias=0.0, scale=1.0, accum=None, sc=None):
        d = vd(width(a))
        r = [a] if sc is None else [a, sc]
        if accum is not None:
            put("run", "s", lambda e: e.activation(ap(o), ap(a), f, bias=bias, scale=scale, accum_out=ap(accum)), r, [o, accum], d)
        else:
            put("run", "s", lambda e: e.activation(ap(o), ap(a), f, bias=bias, scale=scale if sc is None else ap(sc)), r, [o], d)

    def apick(o, win, off):
        put("run", "s", lambda e: e.activation(ap(o), ap(win).indirect(ap(off)), AF.Copy), [win, off], [o], 0.08 + 16 * width(off) * G * CY)

    def mm(o, l, r, st, sp):
        put("run", "p", lambda e: e.matmul(ap(o), ap(l), ap(r), st, sp), [l, r], [o], vd(width(r), 0.9))

    def iota(o, pat, base, cm):
        d = 0.16 + 2 * width(o) * CY
        if SCRATCH[o[0]][2] != "int32":
            put("run", "g", lambda e: e.iota(ap(o), pat, base, cm, allow_small_or_imprecise_dtypes=True), [], [o], d)
        else:
            put("run", "g", lambda e: e.iota(ap(o), pat, base, cm), [], [o], d)

    def sift(o, a, pat, op, fill, base, cm):
        put("run", "g", lambda e: e.affine_select(ap(o), ap(a), pat, op, fill, base, cm), [a], [o], 0.2 + 2 * width(o) * CY)

    def load(q, o, a, sem, dur):
        put("dma", q, lambda e: e.dma_start(ap(o), T[a][:]), [], [o], dur, sem=sem)

    def send(m, t):
        where[(m, t)] = len(ops)
        put("send", "g", None, [B("s%s%d" % (m, t))], [], 0.8, msg=(m, t))

    def expect(m, t):
        put("land", None, None, [], [B("l%s%d" % (m, t))], LAT[m], [where[(m, t)]], msg=(m, t))

    load("y", B("entx"), "ent", "ld0", 4.5)
    ms(B("fx", 0, 16), 0.0)
    load("s", B("wti"), "wt", "ld1", 2.2)
    load("s", B("kpi"), "kap", "ld2", 2.2)
    load("y", B("fx", 1, 2049), "feat", "ld3", 6.0)
    ms(B("one"), 1.0)
    sift(B("blka"), B("one"), [[-16, 8], [0, 16]], ALU.is_ge, 0.0, 0, 1)
    sift(B("blk"), B("blka"), [[16, 8], [0, 16]], ALU.is_ge, 0.0, 15, -1)
    iota(B("pmi"), [[0, 16]], 0, 1)
    iota(B("lio"), [[0, 32], [1, 16]], 0, 0)
    iota(B("x16"), [[1, 16]], 0, 0)
    iota(B("mio"), [[1, 16], [0, 16]], 0, 0)
    iota(B("lbl"), [[1, 256]], 1024, 0)
    iota(B("ci"), [[37, 1024]], -1, 0)
    iota(B("iot"), [[1, 1024]], 0, 0)
    ms(B("wsel"), 0.0)
    ms(B("sel"), 0.0)
    ms(B("zer"), 0.0)
    ms(B("allf"), 2.0 ** -28)
    ts(B("sgm"), B("lio"), 1.0, ALU.min)
    ts(B("pmj"), B("pmi"), 15, ALU.bitwise_and)
    cp(B("pmf"), B("pmj"))
    cp(B("wtf"), B("wti"))
    for t in range(NR):
        cp(B("sa%d" % t, 256, 257), B("kpi"))
        cp(B("sa%d" % t, 257, 258), B("kpi"))
    for p in range(16):
        act(B("wsel", 129 * p, 129 * p + 113, 16), B("blk", 0, 113, 16), AF.Copy, sc=B("wtf"))
    act(B("blkb"), B("blk"), AF.Copy, scale=P24)
    for p in range(16):
        act(B("sel", 129 * p, 129 * p + 113, 16), B("blk", 0, 113, 16), AF.Copy, scale=-4096.0)
    ts(B("cmk"), B("x16"), None, ALU.is_gt, P24, ALU.mult, sc=B("pmf", 0, 1))
    for x in range(16):
        act(B("tri", 128 * x, 128 * x + 128), B("blk"), AF.Copy, sc=B("cmk", x, x + 1))
    ts(B("dlt"), B("mio"), None, ALU.is_equal, sc=B("pmf", 0, 1))
    ts(B("c15"), B("pmf", 0, 1), -256.0, ALU.mult, 3840.0, ALU.add)
    ts(B("rA"), B("dlt"), None, ALU.mult, sc=B("c15"))
    ts(B("dma_"), B("lio", 0, 256), None, ALU.is_equal, sc=B("pmf", 0, 1))
    tt(B("DM"), B("dma_"), B("lbl"), ALU.mult)
    cp(B("lst"), B("pmj"))
    ts(B("ci2"), B("ci"), 63, ALU.bitwise_and)
    ts(B("Ct0"), B("ci2"), 4096.0, ALU.mult, 22.0, ALU.add)
    for t in range(1, NR):
        act(B("Ct%d" % t), B("Ct0"), AF.Identity, bias=float(t))

    def lanes(c):
        return ("R", c, 1021 + c, 4)

    def convert(c):
        x = B("entx", c, 1021 + c, 4)
        v, w = ("v1", "v3") if c % 2 else ("v2", "v5")
        ts(B("xv"), x, 2047.0, ALU.add)
        ts(B("xh"), B("xv"), -2048, ALU.bitwise_and)
        ts(B(v), B("xh"), 3.0, ALU.mult)
        tt(B("xs"), B(v), x, ALU.subtract)
        ts(B(w), B("xs"), 0.0, ALU.is_equal, EMP, ALU.mult)
        tt(lanes(c), B(w), B("xs"), ALU.max)

    def own(t):
        expect("n", t)
        ts(B("v1"), lanes(t), 0.0, ALU.is_equal, P24, ALU.mult)
        tt(B("v3"), B("v1"), B("ln%d" % t), ALU.min)
        tt(lanes(t), B("v3"), lanes(t), ALU.max)

    convert(0)
    FX = B("fx", 0, 2049)
    RT = B("R", 0, 1024)
    for t in range(NR):
        sa, la, su, lu = "sa%d" % t, "la%d" % t, "su%d" % t, "lu%d" % t
        Ct = B("Ct%d" % t)
        cp(B(sa, 0, 256), lanes(t))
        send("a", t)
        for h in range(2):
            lo, hi = 128 * h, 128 * h + 128
            x = ("R", 4 * lo + t, 4 * hi - 3 + t, 4)
            ts(B("k1", lo, hi), x, 16, ALU.bitwise_and)
            tt(B("pr", lo, hi), x, B("k1", lo, hi), ALU.mult)
            ts(B("off", lo, hi), B("pr", lo, hi), 2.0 ** -16, ALU.mult)
        for c in range(8):
            (apick if c < GS else pick)(B("Yg", 512 * c, 512 * c + 512), FX, B("off", 32 * c, 32 * c + 32))
        for c in range(8):
            scan(B("Ys", 512 * c, 512 * c + 512), B("sgm"), B("Yg", 512 * c, 512 * c + 512))
        for p in range(16):
            mm(B("pu", 0, 16), B("wsel", 128 * p, 128 * p + 128), B("Ys", 16 * p + 15, 4096, 256), p == 0, p == 15)
        cp(B("ui"), B("pu", 0, 16))
        ts(B("ub"), B("ui"), 4095, ALU.bitwise_and)
        tt(B("uq"), B("ub"), B("ub"), ALU.mult)
        cp(B(su, 0, 16), B("ub"))
        ts(B("us"), B("uq"), 5, ALU.arith_shift_right)
        if t == 0:
            cp(B(su, 16, 32), B("us"))
        else:
            expect("c", t - 1)
            cp(B("acol"), B("lc%d" % (t - 1)))
            ts(B(su, 16, 32), B("us"), None, ALU.add, sc=B("acol"))
        send("u", t)
        if t == 0:
            for c in range(1, 4):
                convert(c)
        else:
            own(t - 1)
        expect("a", t)
        A = B(la, 0, 256)
        ts(B("oc", 0, 256), A, -16, ALU.bitwise_and)
        put("dma", "y", lambda e: e.dma_start(T.oc[:, 256:512], T.oc[:, 0:256]), [B("oc", 0, 256)], [B("oc", 256, 512)], 2.2, sem="oc%d" % t)
        cp(B("kcol"), B(la, 256, 257))
        ts(B("rK"), B("dlt"), None, ALU.mult, sc=B("kcol"))
        mm(B("pm", 0, 256), B("blk"), B("rK"), True, True)
        act(B("KM"), B("pm", 0, 256), AF.Copy)
        act(B("ctl"), ("Ct%d" % t, t, 1021 + t, 4), AF.Copy)
        tt(B("qa"), B("ctl"), A, ALU.add)
        ts(B("za"), B("qa"), 0x3801F, ALU.bitwise_and)
        ts(B("l5a"), B("qa"), 31, ALU.bitwise_and)
        ts(B("v5"), B("l5a"), float(5 + t), ALU.is_le, EMP, ALU.mult)
        ts(B("v6"), B("za"), float(5 + t), ALU.is_gt, P24, ALU.mult)
        tt(B("aw"), B("v5"), A, ALU.max)
        tt(B("v4"), B("v6"), A, ALU.add)
        tt(B("aP"), B("v4"), B("aw"), ALU.min)
        tt(B("zda"), B("v6"), B("za"), ALU.subtract)
        act(B("dap"), B("zda"), AF.Relu, bias=7.0 / 16, scale=-1.0 / 16)
        act(B("ca"), B("aP"), AF.Identity, bias=EMP * 2048.0, scale=-2048.0)
        ts(B("ita"), A, 16, ALU.bitwise_and)
        expect("u", t)
        u, s = B(lu, 0, 16), B(lu, 16, 32)
        for h in range(PIECES):
            lo, hi = 256 * h // PIECES, 256 * (h + 1) // PIECES
            pick(B("ep", lo, hi), u, B("lst", lo // 16, hi // 16), B("KM", lo, hi), ALU.mult)
            pick(B("ei", lo, hi), s, B("lst", lo // 16, hi // 16), B("ep", lo, hi), ALU.add)
            ts(B("em", lo, hi), B("ei", lo, hi), 1023, ALU.bitwise_and)
            cp(B("eu", lo, hi), B("em", lo, hi))

        def ch(n, c):
            return B(n, 512 * c, 512 * c + 512)
        for c in range(8):
            pick(ch("D", c), RT, B("eu", 32 * c, 32 * c + 32), B("oc"), ALU.subtract)
            act(ch("X", c), ch("D", c), AF.Abs, bias=-7.5)
            ts(ch("Y", c), ch("X", c), 3000.0, ALU.min, 262144.0 + 1016.0, ALU.add)
            if c < SQ:
                act(ch("NM", c), ch("Y", c), AF.Square, bias=-129.0, scale=2.0 ** -11)
            else:
                ts(ch("NM", c), ch("Y", c), 262144.0 + 2048.0, ALU.not_equal)
        for c in range(4):
            o = B("pk%d" % (c % 2), 0, 64)
            mm(o, B("blk"), B("rA", 64 * c, 64 * c + 64), True, False)
            mm(o, B("blk"), B("rK", 64 * c, 64 * c + 64), False, False)
            for p in range(16):
                mm(o, B("sel", 128 * p, 128 * p + 128), B("NM", 1024 * c + p, 1024 * c + 1024, 16), False, p == 15)
            if c == 0:
                cp(B("mx"), o)
            else:
                tt(B("mx"), o, B("mx"), ALU.max)
        tt(B("m2"), B("mx", 0, 32), B("mx", 32, 64), ALU.max)
        tt(B("ky"), B("m2", 0, 16), B("m2", 16, 32), ALU.max)
        ts(B("kk"), B("ky"), 255, ALU.bitwise_and)
        tt(B("ku"), u, B("kk"), ALU.mult)
        tt(B("es"), s, B("ku"), ALU.add)
        ts(B("er"), B("es"), 1023, ALU.bitwise_and)
        cp(B("e16"), B("er"))
        cp(B("erf"), B("er"))
        pc = B("pc", 0, 256)
        pick(B("ebc"), B("iot"), B("e16"))
        mm(pc, B("zer", 0, 128), B("zer"), True, False)
        for k in range(16):
            ts(B("EQ", 256 * k, 240 * k + 256), B("ebc", 16 * k, 256), None, ALU.is_equal, sc=B("erf", k, k + 1))
            if k < 15:
                mm(B("pc", 16 * k + 16, 256), B("blkb"), B("EQ", 256 * k + 16, 240 * k + 256), False, False)
        for x in range(16):
            mm(B("pc", x, 241 + x, 16), B("tri", 128 * x, 128 * x + 128), B("EQ", x, 3841 + x, 256), False, x == 15)
        act(B("wnp"), pc, AF.Relu, bias=P24, scale=-1.0, accum=B("wacc"))
        if t < NR - 1:
            mm(B("pu", 32, 33), B("allf"), B("wacc"), True, True)
            cp(B("ti"), B("pu", 32, 33))
            ts(B("sc%d" % t), B("ti"), 31, ALU.bitwise_and)
            send("c", t)
        pick(B("bI"), RT, B("e16"))
        pick(B("qb"), Ct, B("e16"), B("bI"), ALU.add)
        ts(B("zb"), B("qb"), 0x3801F, ALU.bitwise_and)
        ts(B("l5b"), B("qb"), 31, ALU.bitwise_and)
        ts(B("v1"), B("l5b"), float(5 + t), ALU.is_le, EMP, ALU.mult)
        ts(B("v3"), B("zb"), float(5 + t), ALU.is_gt, P24, ALU.mult)
        tt(B("v2"), B("v1"), B("bI"), ALU.max)
        tt(B("bs"), B("v3"), B("bI"), ALU.add)
        tt(B("bPp"), B("v2"), B("bs"), ALU.min)
        tt(B("dp"), B("bPp"), B("aP"), ALU.subtract)
        act(B("Xd"), B("dp"), AF.Abs)
        act(B("nsp"), B("Xd"), AF.Relu, bias=-2047.5 * P24, scale=P24)
        act(B("cbp"), B("bPp"), AF.Identity, bias=EMP * 2048.0, scale=-2048.0)
        ts(B("itb"), B("bI"), 16, ALU.bitwise_and)
        tt(B("zdb"), B("v3"), B("zb"), ALU.subtract)
        act(B("dbp"), B("zdb"), AF.Relu, bias=7.0 / 16, scale=-1.0 / 16)
        tt(B("pb"), B("dbp"), B("ita"), ALU.mult)
        tt(B("wbx"), B("bPp"), B("pb"), ALU.subtract)
        tt(B("v5"), B("dap"), B("itb"), ALU.mult)
        tt(B("v4"), B("aP"), B("v5"), ALU.subtract)
        tt(B("rr"), B("v4"), B("wbx"), ALU.min)
        tt(B("na1"), B("v2"), B("ca"), ALU.add)
        tt(B("nb1"), B("cbp"), B("aw"), ALU.add)
        tt(B("a1"), B("wnp"), A, ALU.max)
        tt(B("v6"), B("nsp"), B("rr"), ALU.add)
        tt(B("nbA"), B("v6"), B("nb1"), ALU.min)
        tt(B("nb"), B("bPp"), B("nbA"), ALU.min)
        tt(B("v5"), B("v6"), B("aP"), ALU.min)
        tt(B("na3"), B("v5"), B("na1"), ALU.min)
        tt(B("v2"), pc, B("na3"), ALU.max)
        tt(B("sn%d" % t), B("v2"), B("a1"), ALU.min)
        send("n", t)
        tt(B("px"), pc, B("DM"), ALU.min)
        scan(B("ps"), B("sgm", 0, 256), B("px"))
        tt(B("pf"), B("erf"), B("ps", 15, 256, 16), ALU.max)
        cp(B("pos"), B("pf"))
        iota(lanes(t), [[0, 256]], 0, 0)
        scatter(B("R"), B("pos"), B("nb"))

    def decode(c):
        r = lanes(c)
        v, w = ("v1", "v3") if c % 2 else ("v5", "v6")
        ts(B("hi"), r, -4096, ALU.bitwise_and)
        ts(B(w), r, EMP, ALU.is_lt)
        ts(B(v), B("hi"), 1.5, ALU.mult)
        tt(B("xo"), B(v), r, ALU.subtract)
        tt(B("yo", c, 1021 + c, 4), B(w), B("xo"), ALU.mult)
    last = (NR - 1) % 4
    for c in range(4):
        if c != last:
            decode(c)
    own(NR - 1)
    decode(last)
    put("dma", "y", lambda e: e.dma_start(T.yent[:], T.yo[:]), [B("yo")], [], 4.5, sem="st")
    return ops


ORDER = {}


def plan(T):
    if "o" not in ORDER:
        ops = record(T)
        pre = links(ops)
        seq = arrange(ops, pre, WAKE)
        ORDER["o"] = (pre, seq, [ops[i]["msg"] for i in seq if ops[i]["kind"] == "send"])
    return ORDER["o"]


def rank_program(g, core, T, topo):
    rank = T.rank_of(core)
    if rank is None:
        hand_on(g, core, T, topo)
        return
    ops = record(T)
    pre, seq, _ = plan(T)
    eng = {"v": g.vector, "s": g.scalar, "p": g.tensor, "g": g, "y": g.sync}
    cnt = {"v": 0, "s": 0, "p": 0, "g": 0}
    known, snaps, tok, sent = {q: {} for q in eng}, {}, {}, 0
    for i in seq:
        o = ops[i]
        q = o["q"]
        if o["kind"] == "land":
            m, t = o["msg"]
            src = T.cores[source(T, rank, m, t)]
            n = 0
            for rl, lo, hi in route(topo, T, src, core, m, t):
                n += bits(topo.mask(src if rl is None else rl, core))
            tok[i] = ("%s%d" % (m, t), n)
            continue
        need = {}
        for j in pre[i]:
            if ops[j]["kind"] != "send" and not (q == "p" and ops[j]["q"] == "p"):
                need[tok[j][0]] = max(need.get(tok[j][0], 0), tok[j][1])
        for s in sorted(need):
            if known[q].get(s, 0) < need[s]:
                eng[q].wait_ge(T.sem[s], need[s])
                known[q][s] = need[s]
                for s2, v2 in snaps.get((s, need[s]), {}).items():
                    known[q][s2] = max(known[q].get(s2, 0), v2)
        if o["kind"] == "run":
            cnt[q] += 1
            tok[i] = ("q" + q, cnt[q])
            o["fn"](eng[q]).then_inc(T.sem["q" + q], 1)
        elif o["kind"] == "dma":
            tok[i] = (o["sem"], 16)
            o["fn"](eng[q]).then_inc(T.sem[o["sem"]], 16)
        else:
            m, t = o["msg"]
            dst = T.cores[target(T, rank, m, t)]
            s, l, at = T["s" + m], T["l" + m], STEP[m] * t
            for rl, lo, hi in route(topo, T, core, dst, m, t):
                to = dst if rl is None else rl
                rid, pid = topo.addr(to, core)
                mk = topo.mask(core, to)
                g.remote_dma(l[:, at + lo:at + hi], s[:, at + lo:at + hi], T.sem["%s%d" % (m, t)], T.sem.lsem, pid, rid, mk)
                sent += bits(mk)
            continue
        snaps[tok[i]] = dict(known[q])
    g.wait_ge(T.sem.st, 16)
    g.wait_ge(T.sem.lsem, sent)
    for q in "vspg":
        g.wait_ge(T.sem["q" + q], cnt[q])
